import numpy as np, ml_dtypes
CORES = [89,94,345,350]
N = 4
GR, GC = 2, 2
L, KA, KB, F = 4, 2, 2, 64
def setup_inputs(rng):
    return {"a": rng.standard_normal((N, 128, KA * 128), dtype=np.float32).astype(ml_dtypes.bfloat16), "b": rng.standard_normal((N, 128, KB * F), dtype=np.float32).astype(ml_dtypes.bfloat16)}
def setup_inputs_big(rng):
    d = setup_inputs(rng)
    for k in ("a", "b"): d[k] = (d[k].astype(np.float32) * 1024.0).astype(d[k].dtype)
    return d
def setup_inputs_small(rng):
    d = setup_inputs(rng)
    for k in ("a", "b"): d[k] = (d[k].astype(np.float32) * (1 / 1024.0)).astype(d[k].dtype)
    return d
def setup_inputs_apart(rng):
    d = setup_inputs(rng)
    f = (10.0 ** rng.permutation(np.linspace(-1.5, 1.5, N))).astype(np.float32).reshape(N, 1, 1)
    for k in ("a", "b"): d[k] = (d[k].astype(np.float32) * f).astype(d[k].dtype)
    return d
def reference(a, b):
    A, B = a.astype(np.float64), b.astype(np.float64)
    y = np.zeros((N, 128, F))
    for i in range(GR):
        for j in range(GC):
            for k in range(L):
                At = A[i * GC + k // KA][:, 128 * (k % KA):128 * (k % KA) + 128]
                Bt = B[(k // KB) * GC + j][:, F * (k % KB):F * (k % KB) + F]
                y[i * GC + j] += At.T @ Bt
    return {"y": y.astype(ml_dtypes.bfloat16 if a.dtype != np.float64 else np.float64)}

from concourse.bass import DstId, RemoteDMATransfer

HOSTS = 4
GR, GC, F = 2, 2, 64
HALVES = 2
ENG_FIRST = 2
ENG_LAST = 8
ENG_A = 8

SCRATCH = {
    "b_out": ("dram", [HALVES * 128, F], "bfloat16"),
    "relay": ("dram", [128, F], "bfloat16"),
    "a_own": ("sbuf", [128, 256], "bfloat16"),
    "a_nb": ("sbuf", [128, 256], "bfloat16"),
    "b_own": ("sbuf", [128, 2 * F], "bfloat16"),
    "b_far": ("sbuf", [128, HALVES * F], "bfloat16"),
    "acc": ("psum", [128, F], "float32"),
    "y_sb": ("sbuf", [128, F], "bfloat16"),
}
SEMAPHORES = ["staged", "a_in", "b_in", "a_came", "b_came", "half_came", "sent", "summed", "rounded", "stored"]

_CACHE = {}


def _engines(mask, groups, n):
    bits = [1 << k for k in range(mask.bit_length()) if (mask >> k) & 1]
    picked = bits[:: len(bits) // (groups * n)][: groups * n]
    return [sum(picked[x::groups]) for x in range(groups)]


def _plan(T, topo):
    if "plan" in _CACHE:
        return _CACHE["plan"]
    plan = []
    for r, src in enumerate(T.cores):
        i, j = divmod(r, GC)
        dst = T.cores[(GR - 1 - i) * GC + j]
        ways = {}
        for c in range(HOSTS * topo.CORES_PER_HOST):
            if (topo.chip(c) == topo.chip(src) and topo.die(c) == topo.die(src) and c not in T.cores
                    and topo.may_write(src, c) and topo.may_write(c, dst)):
                ways.setdefault(topo.host(c), []).append(c)
        for half, h in enumerate(sorted(ways)[:HALVES]):
            plan.append((src, half, ways[h][i], dst))
    _CACHE["plan"] = plan
    return plan


def rank_program(g, core, T, topo):
    S = T.sem
    plan = _plan(T, topo)

    for src, half, relay, dst in plan:
        if relay != core:
            continue
        rid, pid = topo.addr(dst, core)
        g.wait_ge(S.half_came, ENG_FIRST)
        g.remote_dma(T.b_far[:, F * half:F * half + F], T.relay[:], S.b_came, S.sent, pid, rid,
                     _engines(topo.mask(core, dst), 1, ENG_LAST)[0])
        g.wait_ge(S.sent, ENG_LAST)

    rank = T.rank_of(core)
    if rank is None:
        return
    i, j = divmod(rank, GC)
    nb = T.cores[i * GC + (GC - 1 - j)]
    natural = i == j

    g.sync.dma_start(T.b_out[:], T.b[:]).then_inc(S.staged, 16)
    if natural:
        g.sync.dma_start(T.a_own[:], T.a[:]).then_inc(S.a_in, 16)
        a_loaded = 16
    else:
        for p in range(HALVES):
            g.sync.dma_start(T.a_own[:, 128 * p:128 * p + 128], T.a[64 * p:64 * p + 64, :]).then_inc(S.a_in, 16)
        a_loaded = 16 * HALVES
    g.scalar.wait_ge(S.staged, 16)
    g.scalar.dma_start(T.b_own[:], T.b[:]).then_inc(S.b_in, 16)

    mine = [(half, relay) for src, half, relay, dst in plan if src == core]
    masks = _engines(topo.mask(core, mine[0][1]), len(mine), ENG_FIRST)
    transfers = []
    for half, relay in mine:
        rid, pid = topo.addr(relay, core)
        transfers.append(RemoteDMATransfer(dst_ids=[DstId(rid=rid, pnc=pid)], dma_engine_mask=masks[half],
                                           remote_sem=S.half_came, src=T.b_out[128 * half:128 * half + 128, :],
                                           dst=T.relay[:]))
    g.wait_ge(S.staged, 16)
    g.remote_dma_fused(transfers, local_sem=S.sent)
    rid, pid = topo.addr(nb, core)
    g.wait_ge(S.a_in, a_loaded)
    g.remote_dma(T.a_nb[:], T.a_own[:], S.a_came, S.sent, pid, rid, _engines(topo.mask(core, nb), 1, ENG_A)[0])

    a_near, a_far = (T.a_own, T.a_nb) if natural else (T.a_nb, T.a_own)
    g.tensor.wait_ge(S.b_in, 16)
    if natural:
        g.tensor.wait_ge(S.a_in, a_loaded)
    else:
        g.tensor.wait_ge(S.a_came, ENG_A)
    for t in range(2):
        g.tensor.matmul(T.acc[:], a_near[:, 128 * t:128 * t + 128], T.b_own[:, F * t:F * t + F], t == 0, False)
    if natural:
        g.tensor.wait_ge(S.a_came, ENG_A)
    else:
        g.tensor.wait_ge(S.a_in, a_loaded)
    g.tensor.wait_ge(S.b_came, HALVES * ENG_LAST)
    g.tensor.matmul(T.acc[:], a_far[:, 0:128], T.b_far[:, 0:F], False, False)
    g.tensor.matmul(T.acc[:], a_far[:, 128:256], T.b_far[:, F:2 * F], False, True).then_inc(S.summed, 1)

    g.vector.wait_ge(S.summed, 1)
    g.vector.tensor_copy(T.y_sb[:], T.acc[:]).then_inc(S.rounded, 1)
    g.sync.wait_ge(S.rounded, 1)
    g.sync.dma_start(T.y[:], T.y_sb[:]).then_inc(S.stored, 16)
    g.sync.wait_ge(S.stored, 16)
    g.wait_ge(S.sent, len(mine) * ENG_FIRST + ENG_A)
